import numpy as np
import ml_dtypes


def mxq(x, axis, fmt="e4m3"):
    dtype, down = {"e4m3": (ml_dtypes.float8_e4m3fn, 7), "e5m2": (ml_dtypes.float8_e5m2, 14)}[fmt]
    v = np.moveaxis(np.asarray(x, np.float32).astype(ml_dtypes.bfloat16).astype(np.float64), axis, -1)
    blocks = v.reshape(v.shape[:-1] + (-1, 32))
    amax = np.abs(blocks).max(-1, keepdims=True)
    byte = np.maximum(np.where(amax > 0, np.frexp(amax)[1] - 1 + 127, 0) - down, 1)
    scale = np.exp2(byte - 127.0)
    codes = (blocks / scale).astype(np.float32).astype(dtype).astype(np.float64)
    return np.moveaxis((codes * scale).reshape(v.shape), -1, axis)


WIDE = False


def mx_kscale(k):
    if not WIDE:
        return np.ones(k)
    levels = np.array([10, -10, 5, -5, 0])
    if k % 512:
        return np.exp2(np.random.permutation(np.resize(levels, k // 32))).repeat(32)
    a = np.empty((k // 512, 16))
    for p in range(k // 512):
        a[p, :8] = np.random.permutation(np.resize(levels, 8))
        for g in range(8):
            far = levels[np.abs(levels - a[p, g]) >= 10]
            a[p, g + 8] = far[np.random.randint(len(far))]
    return np.exp2(a.ravel()).repeat(32)


def f64(x):
    return np.asarray(x).astype(np.float64)


def striped(idx):
    return np.tile(idx.reshape(-1, 16).T, (8, 1)).astype(np.uint16)


def unstriped(offs):
    return offs[:16].T.reshape(-1).astype(np.int64)


E2M1 = np.array([0.0, 0.5, 1.0, 1.5, 2.0, 3.0, 4.0, 6.0, -0.0, -0.5, -1.0, -1.5, -2.0, -3.0, -4.0, -6.0])


def pack_weight(w, fmt):
    k, n = w.shape
    w = f64(np.asarray(w, np.float32).astype(ml_dtypes.bfloat16)).reshape(k // 32, 32, n)
    amax = np.abs(w).max(1)
    if fmt == "e4m3":
        byte = np.frexp(amax)[1] - 1 + 127 - 7
    else:
        mant, ex = np.frexp(amax / 6.0)
        byte = np.where(mant > 0.5, ex, ex - 1) + 127
    byte = np.clip(np.where(amax > 0, byte, 1), 1, 254)
    scaled = (w * np.exp2(127.0 - byte)[:, None, :]).reshape(k, n).astype(np.float32)
    by_word = np.ascontiguousarray(scaled.reshape(k // 512, 128, 4, n).transpose(0, 1, 3, 2))
    if fmt == "e4m3":
        words = by_word.astype(ml_dtypes.float8_e4m3fn).view(np.uint8)
    else:
        c = by_word.astype(ml_dtypes.float4_e2m1fn).view(np.uint8) & 0xF
        words = (c[..., 0::2] | (c[..., 1::2] << 4)).reshape(k // 512, 128, 2 * n)
    return np.ascontiguousarray(words), np.ascontiguousarray(byte.astype(np.uint8).reshape(k // 512, 16, n))


def unpack_weight(words, scales, fmt):
    g, _, n = scales.shape
    words = np.ascontiguousarray(words).reshape(g, 128, n, -1)
    if fmt == "e4m3":
        vals = words.view(ml_dtypes.float8_e4m3fn).astype(np.float64)
    else:
        nib = np.empty((g, 128, n, 4), np.uint8)
        nib[..., 0::2] = words & 0xF
        nib[..., 1::2] = words >> 4
        vals = E2M1[nib]
    vals = vals * np.repeat(np.exp2(scales.astype(np.float64) - 127.0), 8, axis=1)[..., None]
    return vals.transpose(0, 1, 3, 2).reshape(g * 512, n)


def gelu(v):
    return 0.5 * v * (1.0 + np.tanh(np.sqrt(2.0 / np.pi) * (v + 0.044715 * v**3)))


K, H, T, S, P = 1024, 1024, 2048, 1024, 512

def setup_inputs():
    n = np.random.standard_normal
    s = mx_kscale(K)[:, None]
    u = mx_kscale(H)[:, None]
    tab_words, tab_scales = pack_weight(n((K, T)) * s, "e4m3")
    w4_words, w4_scales = pack_weight(1.3 * n((K, H)) / np.sqrt(K) / s, "e2m1")
    return {
        "tab_words": tab_words, "tab_scales": tab_scales,
        "w4_words": w4_words, "w4_scales": w4_scales,
        "w1": (1.2 * n((K, H)) / np.sqrt(K) / np.sqrt(H) / s / u.T).astype(np.float32),
        "bias": (0.5 * n(H)).astype(np.float32),
        "gain": (np.exp(0.3 * n(H)) * u[:, 0]).astype(np.float32),
        "trace": (1.1 * n(H) / np.sqrt(H) / u[:, 0] ** 2).astype(np.float32),
        "review": np.exp(0.4 * n((P, P))).astype(np.float32),
        "offs": striped(np.random.permutation(T)[:S]),
        "pos1": striped(np.random.permutation(S)[:P]),
        "pos2": striped(np.random.permutation(S)[:P]),
    }

def reference(tab_words, tab_scales, w4_words, w4_scales, w1, bias, gain, trace, review, offs, pos1, pos2):
    v = unpack_weight(tab_words, tab_scales, "e4m3")[:, unstriped(offs)]
    w4 = unpack_weight(w4_words, w4_scales, "e2m1")
    t = np.tanh((w4.T @ v) + f64(bias)[:, None])
    h = t * f64(gain)[:, None]
    c = mxq(f64(w1), 0, "e4m3").T @ v
    l1 = unstriped(pos1)
    l2 = unstriped(pos2)
    x1 = mxq(h[:, l1], 0, "e4m3")
    x2 = mxq(np.abs(h[:, l2]) * f64(trace)[:, None], 0, "e4m3")
    c1 = mxq(c[:, l1], 0, "e4m3")
    h2 = mxq(h[:, l2], 0, "e4m3")
    e = x1.T @ x2 + c1.T @ h2
    return np.tanh(e) * f64(review)

@@ -1,0 +1,320 @@
+from contextlib import ExitStack
+
+import concourse.mybir as mybir
+from concourse.masks import make_identity
+
+K, H, T, S, NP = 1024, 1024, 2048, 1024, 512
+FLOPS = 2 * (2 * K * H * S + 2 * H * NP * NP)
+
+F32 = mybir.dt.float32
+BF16 = mybir.dt.bfloat16
+I32 = mybir.dt.int32
+U32 = mybir.dt.uint32
+U16 = mybir.dt.uint16
+U8 = mybir.dt.uint8
+FP8X4 = mybir.dt.float8_e4m3fn_x4
+FP4X4 = mybir.dt.float4_e2m1fn_x4
+ACT = mybir.ActivationFunctionType
+ALU = mybir.AluOpType
+
+P = 128
+PACK = 4
+PASS = P * PACK
+BANK = 512
+PASSES = K // PASS
+GROUPS = H // PASS
+
+
+def tile_list_privilege_taint_scores_kernel(
+    tc, tab_words, tab_scales, w4_words, w4_scales, w1, bias, gain, trace, review, offs, pos1, pos2, out
+):
+    nc = tc.nc
+    with ExitStack() as ctx:
+        keep = ctx.enter_context(tc.tile_pool(name="keep", bufs=1))
+        ring = ctx.enter_context(tc.tile_pool(name="ring", bufs=2))
+        psum = ctx.enter_context(tc.psum_pool(name="psum", bufs=1))
+
+        offs_sb = keep.tile([P, S // 16], U16, name="offs_sb")
+        pos1_sb = keep.tile([P, NP // 16], U16, name="pos1_sb")
+        pos2_sb = keep.tile([P, NP // 16], U16, name="pos2_sb")
+
+        def load_tile(name, shape, dtype, slot):
+            return keep.tile(shape, dtype, name=name, tag="load%d" % slot, align_bytes=64)
+
+        tab_sc = load_tile("tab_sc", [P, T], U8, 0)
+        for quad in range(4):
+            nc.vector.memset(tab_sc[32 * quad : 32 * quad + 24, :].bitcast(I32), 0)
+        w4_sc_raw = keep.tile([P, PASSES * H], U8, name="w4_sc_raw", align_bytes=64)
+        nc.gpsimd.memset(w4_sc_raw[:].bitcast(I32), 0)
+        rows = keep.tile([P, GROUPS * P], F32, name="rows", align_bytes=64)
+        nc.gpsimd.memset(rows[:], 0.0)
+        v_scales = [keep.tile([P, S], U8, name="v_sc%d" % a, align_bytes=64) for a in range(PASSES)]
+        for a in range(PASSES):
+            nc.vector.memset(v_scales[a][96:128, :].bitcast(I32), 0)
+
+        nc.sync.dma_start(offs_sb[:], offs)
+        for quad in range(4):
+            nc.sync.dma_start(
+                tab_sc[32 * quad + 24 : 32 * quad + 32, :].bitcast(I32),
+                tab_scales[:, 4 * quad : 4 * quad + 4, :].bitcast(I32),
+            )
+        tab_w = [load_tile("tab_w%d" % a, [P, T], U32, 1 + 2 * a) for a in range(PASSES)]
+
+        def load_table(a):
+            nc.sync.dma_start(
+                tab_w[a][:].bitcast(I32), tab_words[a].rearrange("p t i -> p (t i)").bitcast(I32)
+            )
+
+        def load_row(v, vec):
+            nc.gpsimd.dma_start(
+                rows[PACK * v : PACK * (v + 1), :].rearrange("t (g e) -> t g e", e=4),
+                vec.rearrange("(g t e) -> t g e", t=PACK, e=4),
+            )
+
+        load_row(0, bias)
+        load_row(1, gain)
+        load_row(2, trace)
+        load_table(0)
+        nc.sync.dma_start(pos1_sb[:], pos1)
+        nc.sync.dma_start(pos2_sb[:], pos2)
+        w4_raw = load_tile("w4_raw", [P, PASSES, H // 2], I32, 2)
+        nc.sync.dma_start(w4_raw[:], w4_words.bitcast(I32).rearrange("a p w -> p a w"))
+        for quad in range(4):
+            nc.sync.dma_start(
+                w4_sc_raw[32 * quad : 32 * quad + 4, :].bitcast(I32).rearrange("r (a w) -> r a w", a=PASSES),
+                w4_scales[:, 4 * quad : 4 * quad + 4, :].bitcast(I32).rearrange("a r w -> r a w"),
+            )
+        load_table(1)
+
+        def planes_tile(name):
+            return ring.tile([P, PACK, BANK], F32, name=name, tag="planes", bufs=6, align_bytes=64)
+
+        w1_raw = {}
+
+        def load_w1(a, b):
+            w1_raw[a, b] = load_tile("w1_raw%d%d" % (a, b), [P, PACK, BANK], F32, a + PASSES * b)
+            nc.sync.dma_start(
+                w1_raw[a, b][:],
+                w1[a * PASS : (a + 1) * PASS, b * PASS : (b + 1) * PASS].rearrange("(p j) c -> p j c", j=PACK),
+            )
+
+        ident = keep.tile([P, P], F32, name="ident", align_bytes=64)
+        make_identity(nc, ident[:])
+        turned = psum.tile([P, BANK], F32, name="turned", tag="stage1", bufs=4)
+        for b in range(GROUPS):
+            nc.tensor.transpose(turned[:, b * P : (b + 1) * P], rows[:, b * P : (b + 1) * P], ident[:])
+
+        v_sc = keep.tile([P, S], U8, name="v_sc", align_bytes=64)
+        nc.vector.tensor_copy(v_sc[:], tab_sc[:].indirect(offs_sb[:]))
+        for a in range(PASSES):
+            nc.scalar.dma_start(
+                v_scales[a][0:100, :].bitcast(I32), v_sc[24 + 4 * a : 124 + 4 * a, :].bitcast(I32)
+            )
+        load_w1(0, 0)
+        v_w = [
+            [keep.tile([P, BANK], U32, name="v_w%d%d" % (a, n), align_bytes=64) for n in range(S // BANK)]
+            for a in range(PASSES)
+        ]
+
+        def gather_table(a):
+            for n in range(S // BANK):
+                nc.vector.tensor_copy(v_w[a][n][:], tab_w[a][:].indirect(offs_sb[:, 32 * n : 32 * (n + 1)]))
+
+        gather_table(0)
+        load_w1(1, 0)
+        w4_w = keep.tile([P, PASSES * H // 2], I32, name="w4_w", align_bytes=64)
+        nc.vector.tensor_copy(
+            w4_w[:].rearrange("p (g t q h) -> p g t q h", t=PACK, q=32, h=2),
+            w4_raw[:].rearrange("p a (b q t h) -> p (a b) t q h", t=PACK, q=32, h=2),
+        )
+        load_w1(0, 1)
+        w4_sc = keep.tile([P, PASSES * H], U8, name="w4_sc", align_bytes=64)
+        nc.vector.tensor_copy(
+            w4_sc[:].bitcast(I32).rearrange("p (g t q) -> p g t q", t=PACK, q=32),
+            w4_sc_raw[:].bitcast(I32).rearrange("p (g q t) -> p g t q", t=PACK, q=32),
+        )
+        gather_table(1)
+        load_w1(1, 1)
+        consts = keep.tile([P, GROUPS, 3 * PACK], F32, name="consts", align_bytes=64)
+        nc.vector.tensor_copy(
+            consts[:], turned[:, 0 : GROUPS * P].rearrange("p (b c) -> p b c", b=GROUPS)[:, :, 0 : 3 * PACK]
+        )
+
+        def rounded_tile(name):
+            return ring.tile([P, PACK * BANK], BF16, name=name, tag="rounded", bufs=6, align_bytes=64)
+
+        def mx_tiles(name):
+            return (
+                keep.tile([P, BANK], U32, name=name + "_w", align_bytes=64),
+                keep.tile([P, BANK], U8, name=name + "_s", align_bytes=64),
+            )
+
+        def quantize(mx, rounded, c0=0, c1=BANK):
+            nc.vector.quantize_mx(
+                out=mx[0][:, c0:c1].bitcast(FP8X4), scales=mx[1][:, c0:c1], in_=rounded[:, PACK * c0 : PACK * c1]
+            )
+
+        w1_mx = {}
+
+        def prepare_w1(a, b, copy):
+            rounded = rounded_tile("w1_bf%d%d" % (a, b))
+            copy(
+                rounded[:].rearrange("p (t q e j) -> p t q j e", t=PACK, e=4, j=PACK),
+                w1_raw[a, b][:].rearrange("p j (q t e) -> p t q j e", t=PACK, e=4),
+            )
+            return rounded
+
+        def quantize_w1(a, b, rounded):
+            w1_mx[a, b] = mx_tiles("w1_mx%d%d" % (a, b))
+            quantize(w1_mx[a, b], rounded)
+
+        def stage1(b, t, operand):
+            banks = []
+            for n in range(S // BANK):
+                bank = psum.tile([P, BANK], F32, name="bank", tag="stage1", bufs=4)
+                for a in range(PASSES):
+                    words, scales = operand(a, b, t)
+                    nc.tensor.matmul_mx(
+                        out=bank[:],
+                        lhsT=words,
+                        lhsT_scale=scales,
+                        rhs=v_w[a][n][:].bitcast(FP8X4),
+                        rhs_scale=v_scales[a][:, n * BANK : (n + 1) * BANK],
+                        start=(a == 0),
+                        stop=(a == PASSES - 1),
+                    )
+                banks.append(bank)
+            return banks
+
+        def w4_operand(a, b, t):
+            c0 = a * H + b * PASS + t * P
+            return w4_w[:].bitcast(U8)[:, 2 * c0 : 2 * (c0 + P)].bitcast(FP4X4), w4_sc[:, c0 : c0 + P]
+
+        def w1_operand(a, b, t):
+            words, scales = w1_mx[a, b]
+            return words[:, t * P : (t + 1) * P].bitcast(FP8X4), scales[:, t * P : (t + 1) * P]
+
+        h1_planes, h2_planes, c1_planes, c_rows = {}, {}, {}, {}
+
+        def h_tile(b, t):
+            if t == 0:
+                h1_planes[b] = planes_tile("h1_planes%d" % b)
+                h2_planes[b] = planes_tile("h2_planes%d" % b)
+            banks = stage1(b, t, w4_operand)
+            tanh_rows = ring.tile([P, S], F32, name="tanh_rows", tag="rows", bufs=10, align_bytes=64)
+            for n, bank in enumerate(banks):
+                nc.scalar.activation(
+                    tanh_rows[:, n * BANK : (n + 1) * BANK], bank[:], ACT.Tanh, bias=consts[:, b, t : t + 1]
+                )
+            h_rows = ring.tile([P, S], F32, name="h_rows", bufs=2, align_bytes=64)
+            nc.vector.tensor_scalar(
+                h_rows[:], tanh_rows[:], consts[:, b, PACK + t : PACK + t + 1], None, ALU.mult
+            )
+            nc.vector.tensor_copy(h1_planes[b][:, t, :], h_rows[:].indirect(pos1_sb[:]))
+            nc.vector.tensor_copy(h2_planes[b][:, t, :], h_rows[:].indirect(pos2_sb[:]))
+
+        def c_tile(b, t):
+            banks = stage1(b, t, w1_operand)
+            c_rows[b, t] = ring.tile([P, S], F32, name="c_rows", tag="rows", bufs=10, align_bytes=64)
+            for n, bank in enumerate(banks):
+                nc.scalar.copy(c_rows[b, t][:, n * BANK : (n + 1) * BANK], bank[:])
+
+        def c_gather(b, t, m0=0, m1=NP):
+            if b not in c1_planes:
+                c1_planes[b] = planes_tile("c1_planes%d" % b)
+            nc.vector.tensor_copy(
+                c1_planes[b][:, t, m0:m1], c_rows[b, t][:].indirect(pos1_sb[:, m0 // 16 : m1 // 16])
+            )
+
+        def woven(tile, c0=0, c1=BANK):
+            return tile[:, PACK * c0 : PACK * c1].rearrange("p (c i t) -> p c t i", i=4, t=PACK)
+
+        def by_fours(planes, c0=0, c1=BANK):
+            return planes[:, :, c0:c1].rearrange("p t (c i) -> p c t i", i=4)
+
+        x1_mx, x2_mx, h2_mx, c1_mx = {}, {}, {}, {}
+
+        def h_operands(b):
+            magnitude = load_tile("magnitude", [P, PACK * BANK], F32, 3)
+            nc.scalar.activation(woven(magnitude), by_fours(h2_planes[b]), ACT.Abs)
+            x2 = rounded_tile("x2_bf%d" % b)
+            nc.vector.tensor_tensor(
+                x2[:].rearrange("p (m t) -> p m t", t=PACK),
+                magnitude[:].rearrange("p (m t) -> p m t", t=PACK),
+                consts[:, b, 2 * PACK : 3 * PACK].unsqueeze(1).to_broadcast([P, BANK, PACK]),
+                ALU.mult,
+            )
+            h2 = rounded_tile("h2_bf%d" % b)
+            nc.scalar.copy(woven(h2), by_fours(h2_planes[b]))
+            x1 = rounded_tile("x1_bf%d" % b)
+            nc.scalar.copy(woven(x1), by_fours(h1_planes[b]))
+            x2_mx[b], h2_mx[b], x1_mx[b] = mx_tiles("x2_mx%d" % b), mx_tiles("h2_mx%d" % b), mx_tiles("x1_mx%d" % b)
+            quantize(x2_mx[b], x2)
+            quantize(h2_mx[b], h2)
+            quantize(x1_mx[b], x1)
+
+        scores = [psum.tile([P, NP], F32, name="scores%d" % mt) for mt in range(NP // P)]
+
+        def stage2(mt, left, right, start, stop):
+            nc.tensor.matmul_mx(
+                out=scores[mt][:],
+                lhsT=left[0][:, mt * P : (mt + 1) * P].bitcast(FP8X4),
+                lhsT_scale=left[1][:, mt * P : (mt + 1) * P],
+                rhs=right[0][:].bitcast(FP8X4),
+                rhs_scale=right[1][:],
+                start=start,
+                stop=stop,
+            )
+
+        def finish(mt):
+            squashed = ring.tile([P, NP], F32, name="squashed", bufs=2, align_bytes=64)
+            nc.scalar.activation(squashed[:], scores[mt][:], ACT.Tanh)
+            result = ring.tile([P, NP], F32, name="result", bufs=2, align_bytes=64)
+            nc.vector.tensor_tensor(result[:], squashed[:], review_sb[:, mt, :], ALU.mult)
+            nc.sync.dma_start(out[mt * P : (mt + 1) * P, :], result[:])
+
+        first = prepare_w1(0, 0, nc.vector.tensor_copy)
+        review_sb = load_tile("review_sb", [P, NP // P, NP], F32, 0)
+        nc.sync.dma_start(review_sb[:], review.rearrange("(mt p) j -> p mt j", p=P))
+        h_tile(0, 0)
+        quantize_w1(0, 0, first)
+        h_tile(0, 1)
+        quantize_w1(1, 0, prepare_w1(1, 0, nc.scalar.copy))
+        h_tile(0, 2)
+        h_tile(0, 3)
+        quantize_w1(0, 1, prepare_w1(0, 1, nc.scalar.copy))
+        h_tile(1, 0)
+        quantize_w1(1, 1, prepare_w1(1, 1, nc.scalar.copy))
+        h_tile(1, 1)
+        c_tile(0, 0)
+        c_tile(0, 1)
+        h_tile(1, 2)
+        c_tile(0, 2)
+        c_tile(0, 3)
+        h_tile(1, 3)
+        h_operands(0)
+        for t in range(PACK):
+            c_gather(0, t)
+        for t in range(PACK):
+            c_tile(1, t)
+        for mt in range(NP // P):
+            stage2(mt, x1_mx[0], x2_mx[0], True, False)
+        c1 = rounded_tile("c1_bf0")
+        nc.scalar.copy(woven(c1), by_fours(c1_planes[0]))
+        h_operands(1)
+        c1_mx[0] = mx_tiles("c1_mx0")
+        quantize(c1_mx[0], c1)
+        for mt in range(NP // P):
+            stage2(mt, c1_mx[0], h2_mx[0], False, False)
+        for mt in range(NP // P):
+            stage2(mt, x1_mx[1], x2_mx[1], False, False)
+        c1 = rounded_tile("c1_bf1")
+        c1_mx[1] = mx_tiles("c1_mx1")
+        for m0, m1 in ((0, 256), (256, 384), (384, 512)):
+            for t in range(PACK):
+                c_gather(1, t, m0, m1)
+            nc.vector.tensor_copy(woven(c1, m0, m1), by_fours(c1_planes[1], m0, m1))
+            quantize(c1_mx[1], c1, m0, m1)
+            for mt in range(m0 // P, m1 // P):
+                stage2(mt, c1_mx[1], h2_mx[1], False, True)
+                finish(mt)

@@ -58,7 +58,7 @@ def tile_list_privilege_taint_scores_kernel(
                 tab_sc[32 * quad + 24 : 32 * quad + 32, :].bitcast(I32),
                 tab_scales[:, 4 * quad : 4 * quad + 4, :].bitcast(I32),
             )
-        tab_w = [load_tile("tab_w%d" % a, [P, T], U32, 1 + 2 * a) for a in range(PASSES)]
+        tab_w = [load_tile("tab_w%d" % a, [P, T], U32, 1 + a) for a in range(PASSES)]
 
         def load_table(a):
             nc.sync.dma_start(
@@ -77,17 +77,17 @@ def tile_list_privilege_taint_scores_kernel(
         load_table(0)
         nc.sync.dma_start(pos1_sb[:], pos1)
         nc.sync.dma_start(pos2_sb[:], pos2)
-        w4_raw = load_tile("w4_raw", [P, PASSES, H // 2], I32, 2)
+        load_table(1)
+        w4_raw = load_tile("w4_raw", [P, PASSES, H // 2], I32, 3)
         nc.sync.dma_start(w4_raw[:], w4_words.bitcast(I32).rearrange("a p w -> p a w"))
         for quad in range(4):
             nc.sync.dma_start(
                 w4_sc_raw[32 * quad : 32 * quad + 4, :].bitcast(I32).rearrange("r (a w) -> r a w", a=PASSES),
                 w4_scales[:, 4 * quad : 4 * quad + 4, :].bitcast(I32).rearrange("a r w -> r a w"),
             )
-        load_table(1)
 
-        def planes_tile(name):
-            return ring.tile([P, PACK, BANK], F32, name=name, tag="planes", bufs=6, align_bytes=64)
+        def planes_tile(name, tag):
+            return keep.tile([P, PACK, BANK], F32, name=name, tag=tag, align_bytes=64)
 
         w1_raw = {}
 
@@ -110,35 +110,43 @@ def tile_list_privilege_taint_scores_kernel(
             nc.scalar.dma_start(
                 v_scales[a][0:100, :].bitcast(I32), v_sc[24 + 4 * a : 124 + 4 * a, :].bitcast(I32)
             )
-        load_w1(0, 0)
         v_w = [
             [keep.tile([P, BANK], U32, name="v_w%d%d" % (a, n), align_bytes=64) for n in range(S // BANK)]
             for a in range(PASSES)
         ]
 
-        def gather_table(a):
-            for n in range(S // BANK):
-                nc.vector.tensor_copy(v_w[a][n][:], tab_w[a][:].indirect(offs_sb[:, 32 * n : 32 * (n + 1)]))
+        def gather_table(a, n):
+            nc.vector.tensor_copy(v_w[a][n][:], tab_w[a][:].indirect(offs_sb[:, 32 * n : 32 * (n + 1)]))
 
-        gather_table(0)
+        w4_w, w4_sc = {}, {}
+
+        def deal_w4(b):
+            w4_w[b] = keep.tile([P, PASSES, PASS // 2], I32, name="w4_w%d" % b, align_bytes=64)
+            nc.vector.tensor_copy(
+                w4_w[b][:].rearrange("p a (t q h) -> p a q t h", t=PACK, h=2),
+                w4_raw[:, :, b * (PASS // 2) : (b + 1) * (PASS // 2)].rearrange("p a (q t h) -> p a q t h", t=PACK, h=2),
+            )
+            w4_sc[b] = keep.tile([P, PASSES, PASS // 4], I32, name="w4_sc%d" % b, align_bytes=64)
+            nc.vector.tensor_copy(
+                w4_sc[b][:].rearrange("p a (t q) -> p a q t", t=PACK),
+                w4_sc_raw[:].bitcast(I32).rearrange("p (a b q t) -> p b a q t", a=PASSES, b=GROUPS, t=PACK)[:, b],
+            )
+
+        load_w1(0, 0)
+        gather_table(0, 0)
+        gather_table(0, 1)
         load_w1(1, 0)
-        w4_w = keep.tile([P, PASSES * H // 2], I32, name="w4_w", align_bytes=64)
-        nc.vector.tensor_copy(
-            w4_w[:].rearrange("p (g t q h) -> p g t q h", t=PACK, q=32, h=2),
-            w4_raw[:].rearrange("p a (b q t h) -> p (a b) t q h", t=PACK, q=32, h=2),
-        )
+        gather_table(1, 0)
+        deal_w4(0)
+        gather_table(1, 1)
         load_w1(0, 1)
-        w4_sc = keep.tile([P, PASSES * H], U8, name="w4_sc", align_bytes=64)
-        nc.vector.tensor_copy(
-            w4_sc[:].bitcast(I32).rearrange("p (g t q) -> p g t q", t=PACK, q=32),
-            w4_sc_raw[:].bitcast(I32).rearrange("p (g q t) -> p g t q", t=PACK, q=32),
-        )
-        gather_table(1)
-        load_w1(1, 1)
         consts = keep.tile([P, GROUPS, 3 * PACK], F32, name="consts", align_bytes=64)
         nc.vector.tensor_copy(
             consts[:], turned[:, 0 : GROUPS * P].rearrange("p (b c) -> p b c", b=GROUPS)[:, :, 0 : 3 * PACK]
         )
+
+        deal_w4(1)
+        load_w1(1, 1)
 
         def rounded_tile(name):
             return ring.tile([P, PACK * BANK], BF16, name=name, tag="rounded", bufs=6, align_bytes=64)
@@ -168,10 +176,13 @@ def tile_list_privilege_taint_scores_kernel(
             w1_mx[a, b] = mx_tiles("w1_mx%d%d" % (a, b))
             quantize(w1_mx[a, b], rounded)
 
-        def stage1(b, t, operand):
+        def stage1(b, t, operand, late=False):
             banks = []
             for n in range(S // BANK):
-                bank = psum.tile([P, BANK], F32, name="bank", tag="stage1", bufs=4)
+                if late:
+                    bank = psum.tile([P, BANK], F32, name="late_bank", tag="scores%d" % (2 * (t % 2) + n))
+                else:
+                    bank = psum.tile([P, BANK], F32, name="bank", tag="stage1", bufs=4)
                 for a in range(PASSES):
                     words, scales = operand(a, b, t)
                     nc.tensor.matmul_mx(
@@ -187,8 +198,8 @@ def tile_list_privilege_taint_scores_kernel(
             return banks
 
         def w4_operand(a, b, t):
-            c0 = a * H + b * PASS + t * P
-            return w4_w[:].bitcast(U8)[:, 2 * c0 : 2 * (c0 + P)].bitcast(FP4X4), w4_sc[:, c0 : c0 + P]
+            words = w4_w[b][:, a, :].bitcast(U8)[:, 2 * t * P : 2 * (t + 1) * P]
+            return words.bitcast(FP4X4), w4_sc[b][:, a, :].bitcast(U8)[:, t * P : (t + 1) * P]
 
         def w1_operand(a, b, t):
             words, scales = w1_mx[a, b]
@@ -198,30 +209,30 @@ def tile_list_privilege_taint_scores_kernel(
 
         def h_tile(b, t):
             if t == 0:
-                h1_planes[b] = planes_tile("h1_planes%d" % b)
-                h2_planes[b] = planes_tile("h2_planes%d" % b)
+                h1_planes[b] = planes_tile("h1_planes%d" % b, "pos1_planes%d" % b)
+                h2_planes[b] = planes_tile("h2_planes%d" % b, "pos2_planes%d" % b)
             banks = stage1(b, t, w4_operand)
             tanh_rows = ring.tile([P, S], F32, name="tanh_rows", tag="rows", bufs=10, align_bytes=64)
             for n, bank in enumerate(banks):
                 nc.scalar.activation(
                     tanh_rows[:, n * BANK : (n + 1) * BANK], bank[:], ACT.Tanh, bias=consts[:, b, t : t + 1]
                 )
-            h_rows = ring.tile([P, S], F32, name="h_rows", bufs=2, align_bytes=64)
-            nc.vector.tensor_scalar(
-                h_rows[:], tanh_rows[:], consts[:, b, PACK + t : PACK + t + 1], None, ALU.mult
+            h_rows = ring.tile([P, S], F32, name="h_rows", bufs=3, align_bytes=64)
+            nc.gpsimd.tensor_scalar(
+                h_rows[:], tanh_rows[:], consts[:, b, PACK + t : PACK + t + 1], 0.0, ALU.mult, ALU.add
             )
             nc.vector.tensor_copy(h1_planes[b][:, t, :], h_rows[:].indirect(pos1_sb[:]))
             nc.vector.tensor_copy(h2_planes[b][:, t, :], h_rows[:].indirect(pos2_sb[:]))
 
         def c_tile(b, t):
-            banks = stage1(b, t, w1_operand)
+            banks = stage1(b, t, w1_operand, late=(b == 1 and t >= 2))
             c_rows[b, t] = ring.tile([P, S], F32, name="c_rows", tag="rows", bufs=10, align_bytes=64)
             for n, bank in enumerate(banks):
                 nc.scalar.copy(c_rows[b, t][:, n * BANK : (n + 1) * BANK], bank[:])
 
         def c_gather(b, t, m0=0, m1=NP):
             if b not in c1_planes:
-                c1_planes[b] = planes_tile("c1_planes%d" % b)
+                c1_planes[b] = planes_tile("c1_planes%d" % b, "pos1_planes%d" % b)
             nc.vector.tensor_copy(
                 c1_planes[b][:, t, m0:m1], c_rows[b, t][:].indirect(pos1_sb[:, m0 // 16 : m1 // 16])
             )
@@ -234,7 +245,7 @@ def tile_list_privilege_taint_scores_kernel(
 
         x1_mx, x2_mx, h2_mx, c1_mx = {}, {}, {}, {}
 
-        def h_operands(b):
+        def x2_operand(b):
             magnitude = load_tile("magnitude", [P, PACK * BANK], F32, 3)
             nc.scalar.activation(woven(magnitude), by_fours(h2_planes[b]), ACT.Abs)
             x2 = rounded_tile("x2_bf%d" % b)
@@ -244,16 +255,17 @@ def tile_list_privilege_taint_scores_kernel(
                 consts[:, b, 2 * PACK : 3 * PACK].unsqueeze(1).to_broadcast([P, BANK, PACK]),
                 ALU.mult,
             )
-            h2 = rounded_tile("h2_bf%d" % b)
-            nc.scalar.copy(woven(h2), by_fours(h2_planes[b]))
-            x1 = rounded_tile("x1_bf%d" % b)
-            nc.scalar.copy(woven(x1), by_fours(h1_planes[b]))
-            x2_mx[b], h2_mx[b], x1_mx[b] = mx_tiles("x2_mx%d" % b), mx_tiles("h2_mx%d" % b), mx_tiles("x1_mx%d" % b)
+            x2_mx[b] = mx_tiles("x2_mx%d" % b)
             quantize(x2_mx[b], x2)
-            quantize(h2_mx[b], h2)
-            quantize(x1_mx[b], x1)
 
-        scores = [psum.tile([P, NP], F32, name="scores%d" % mt) for mt in range(NP // P)]
+        def plain_operand(name, planes):
+            rounded = rounded_tile(name + "_bf")
+            nc.scalar.copy(woven(rounded), by_fours(planes))
+            mx = mx_tiles(name + "_mx")
+            quantize(mx, rounded)
+            return mx
+
+        scores = {}
 
         def stage2(mt, left, right, start, stop):
             nc.tensor.matmul_mx(
@@ -286,28 +298,27 @@ def tile_list_privilege_taint_scores_kernel(
         h_tile(1, 0)
         quantize_w1(1, 1, prepare_w1(1, 1, nc.scalar.copy))
         h_tile(1, 1)
-        c_tile(0, 0)
-        c_tile(0, 1)
+        x2_operand(0)
+        h2_mx[0] = plain_operand("h2_0", h2_planes[0])
         h_tile(1, 2)
-        c_tile(0, 2)
-        c_tile(0, 3)
+        x1_mx[0] = plain_operand("x1_0", h1_planes[0])
         h_tile(1, 3)
-        h_operands(0)
+        for b in range(GROUPS):
+            for t in range(PACK):
+                c_tile(b, t)
         for t in range(PACK):
             c_gather(0, t)
-        for t in range(PACK):
-            c_tile(1, t)
+        x2_operand(1)
+        h2_mx[1] = plain_operand("h2_1", h2_planes[1])
+        x1_mx[1] = plain_operand("x1_1", h1_planes[1])
+        c1_mx[0] = plain_operand("c1_0", c1_planes[0])
         for mt in range(NP // P):
-            stage2(mt, x1_mx[0], x2_mx[0], True, False)
-        c1 = rounded_tile("c1_bf0")
-        nc.scalar.copy(woven(c1), by_fours(c1_planes[0]))
-        h_operands(1)
-        c1_mx[0] = mx_tiles("c1_mx0")
-        quantize(c1_mx[0], c1)
+            scores[mt] = psum.tile([P, NP], F32, name="scores%d" % mt, tag="scores%d" % mt)
+        for b in range(GROUPS):
+            for mt in range(NP // P):
+                stage2(mt, x1_mx[b], x2_mx[b], b == 0, False)
         for mt in range(NP // P):
             stage2(mt, c1_mx[0], h2_mx[0], False, False)
-        for mt in range(NP // P):
-            stage2(mt, x1_mx[1], x2_mx[1], False, False)
         c1 = rounded_tile("c1_bf1")
         c1_mx[1] = mx_tiles("c1_mx1")
         for m0, m1 in ((0, 256), (256, 384), (384, 512)):

from contextlib import ExitStack

import concourse.mybir as mybir
from concourse.masks import make_identity

K, H, T, S, NP = 1024, 1024, 2048, 1024, 512
FLOPS = 2 * (2 * K * H * S + 2 * H * NP * NP)

F32 = mybir.dt.float32
BF16 = mybir.dt.bfloat16
I32 = mybir.dt.int32
U32 = mybir.dt.uint32
U16 = mybir.dt.uint16
U8 = mybir.dt.uint8
FP8X4 = mybir.dt.float8_e4m3fn_x4
FP4X4 = mybir.dt.float4_e2m1fn_x4
ACT = mybir.ActivationFunctionType
ALU = mybir.AluOpType

P = 128
PACK = 4
PASS = P * PACK
BANK = 512
PASSES = K // PASS
GROUPS = H // PASS


def tile_list_privilege_taint_scores_kernel(
    tc, tab_words, tab_scales, w4_words, w4_scales, w1, bias, gain, trace, review, offs, pos1, pos2, out
):
    nc = tc.nc
    with ExitStack() as ctx:
        keep = ctx.enter_context(tc.tile_pool(name="keep", bufs=1))
        ring = ctx.enter_context(tc.tile_pool(name="ring", bufs=2))
        psum = ctx.enter_context(tc.psum_pool(name="psum", bufs=1))

        offs_sb = keep.tile([P, S // 16], U16, name="offs_sb")
        pos1_sb = keep.tile([P, NP // 16], U16, name="pos1_sb")
        pos2_sb = keep.tile([P, NP // 16], U16, name="pos2_sb")

        def load_tile(name, shape, dtype, slot):
            return keep.tile(shape, dtype, name=name, tag="load%d" % slot, align_bytes=64)

        tab_sc = load_tile("tab_sc", [P, T], U8, 0)
        for quad in range(4):
            nc.vector.memset(tab_sc[32 * quad : 32 * quad + 24, :].bitcast(I32), 0)
        w4_sc_raw = keep.tile([P, PASSES * H], U8, name="w4_sc_raw", align_bytes=64)
        nc.gpsimd.memset(w4_sc_raw[:].bitcast(I32), 0)
        rows = keep.tile([P, GROUPS * P], F32, name="rows", align_bytes=64)
        nc.gpsimd.memset(rows[:], 0.0)
        v_scales = [keep.tile([P, S], U8, name="v_sc%d" % a, align_bytes=64) for a in range(PASSES)]
        for a in range(PASSES):
            nc.vector.memset(v_scales[a][96:128, :].bitcast(I32), 0)

        nc.sync.dma_start(offs_sb[:], offs)
        for quad in range(4):
            nc.sync.dma_start(
                tab_sc[32 * quad + 24 : 32 * quad + 32, :].bitcast(I32),
                tab_scales[:, 4 * quad : 4 * quad + 4, :].bitcast(I32),
            )
        tab_w = [load_tile("tab_w%d" % a, [P, T], U32, 1 + a) for a in range(PASSES)]

        def load_table(a):
            nc.sync.dma_start(
                tab_w[a][:].bitcast(I32), tab_words[a].rearrange("p t i -> p (t i)").bitcast(I32)
            )

        def load_row(v, vec):
            nc.gpsimd.dma_start(
                rows[PACK * v : PACK * (v + 1), :].rearrange("t (g e) -> t g e", e=4),
                vec.rearrange("(g t e) -> t g e", t=PACK, e=4),
            )

        load_row(0, bias)
        load_row(1, gain)
        load_row(2, trace)
        load_table(0)
        nc.sync.dma_start(pos1_sb[:], pos1)
        nc.sync.dma_start(pos2_sb[:], pos2)
        load_table(1)
        w4_raw = load_tile("w4_raw", [P, PASSES, H // 2], I32, 3)
        nc.sync.dma_start(w4_raw[:], w4_words.bitcast(I32).rearrange("a p w -> p a w"))
        for quad in range(4):
            nc.sync.dma_start(
                w4_sc_raw[32 * quad : 32 * quad + 4, :].bitcast(I32).rearrange("r (a w) -> r a w", a=PASSES),
                w4_scales[:, 4 * quad : 4 * quad + 4, :].bitcast(I32).rearrange("a r w -> r a w"),
            )

        def planes_tile(name, tag):
            return keep.tile([P, PACK, BANK], F32, name=name, tag=tag, align_bytes=64)

        w1_raw = {}

        def load_w1(a, b):
            w1_raw[a, b] = load_tile("w1_raw%d%d" % (a, b), [P, PACK, BANK], F32, a + PASSES * b)
            nc.sync.dma_start(
                w1_raw[a, b][:],
                w1[a * PASS : (a + 1) * PASS, b * PASS : (b + 1) * PASS].rearrange("(p j) c -> p j c", j=PACK),
            )

        ident = keep.tile([P, P], F32, name="ident", align_bytes=64)
        make_identity(nc, ident[:])
        turned = psum.tile([P, BANK], F32, name="turned", tag="stage1", bufs=4)
        for b in range(GROUPS):
            nc.tensor.transpose(turned[:, b * P : (b + 1) * P], rows[:, b * P : (b + 1) * P], ident[:])

        v_sc = keep.tile([P, S], U8, name="v_sc", align_bytes=64)
        nc.vector.tensor_copy(v_sc[:], tab_sc[:].indirect(offs_sb[:]))
        for a in range(PASSES):
            nc.scalar.dma_start(
                v_scales[a][0:100, :].bitcast(I32), v_sc[24 + 4 * a : 124 + 4 * a, :].bitcast(I32)
            )
        v_w = [
            [keep.tile([P, BANK], U32, name="v_w%d%d" % (a, n), align_bytes=64) for n in range(S // BANK)]
            for a in range(PASSES)
        ]

        def gather_table(a, n):
            nc.vector.tensor_copy(v_w[a][n][:], tab_w[a][:].indirect(offs_sb[:, 32 * n : 32 * (n + 1)]))

        w4_w, w4_sc = {}, {}

        def deal_w4(b):
            w4_w[b] = keep.tile([P, PASSES, PASS // 2], I32, name="w4_w%d" % b, align_bytes=64)
            nc.vector.tensor_copy(
                w4_w[b][:].rearrange("p a (t q h) -> p a q t h", t=PACK, h=2),
                w4_raw[:, :, b * (PASS // 2) : (b + 1) * (PASS // 2)].rearrange("p a (q t h) -> p a q t h", t=PACK, h=2),
            )
            w4_sc[b] = keep.tile([P, PASSES, PASS // 4], I32, name="w4_sc%d" % b, align_bytes=64)
            nc.vector.tensor_copy(
                w4_sc[b][:].rearrange("p a (t q) -> p a q t", t=PACK),
                w4_sc_raw[:].bitcast(I32).rearrange("p (a b q t) -> p b a q t", a=PASSES, b=GROUPS, t=PACK)[:, b],
            )

        load_w1(0, 0)
        gather_table(0, 0)
        gather_table(0, 1)
        load_w1(1, 0)
        gather_table(1, 0)
        deal_w4(0)
        gather_table(1, 1)
        load_w1(0, 1)
        consts = keep.tile([P, GROUPS, 3 * PACK], F32, name="consts", align_bytes=64)
        nc.vector.tensor_copy(
            consts[:], turned[:, 0 : GROUPS * P].rearrange("p (b c) -> p b c", b=GROUPS)[:, :, 0 : 3 * PACK]
        )

        deal_w4(1)
        load_w1(1, 1)

        def rounded_tile(name):
            return ring.tile([P, PACK * BANK], BF16, name=name, tag="rounded", bufs=6, align_bytes=64)

        def mx_tiles(name):
            return (
                keep.tile([P, BANK], U32, name=name + "_w", align_bytes=64),
                keep.tile([P, BANK], U8, name=name + "_s", align_bytes=64),
            )

        def quantize(mx, rounded, c0=0, c1=BANK):
            nc.vector.quantize_mx(
                out=mx[0][:, c0:c1].bitcast(FP8X4), scales=mx[1][:, c0:c1], in_=rounded[:, PACK * c0 : PACK * c1]
            )

        w1_mx = {}

        def prepare_w1(a, b, copy):
            rounded = rounded_tile("w1_bf%d%d" % (a, b))
            copy(
                rounded[:].rearrange("p (t q e j) -> p t q j e", t=PACK, e=4, j=PACK),
                w1_raw[a, b][:].rearrange("p j (q t e) -> p t q j e", t=PACK, e=4),
            )
            return rounded

        def quantize_w1(a, b, rounded):
            w1_mx[a, b] = mx_tiles("w1_mx%d%d" % (a, b))
            quantize(w1_mx[a, b], rounded)

        def stage1(b, t, operand, late=False):
            banks = []
            for n in range(S // BANK):
                if late:
                    bank = psum.tile([P, BANK], F32, name="late_bank", tag="scores%d" % (2 * (t % 2) + n))
                else:
                    bank = psum.tile([P, BANK], F32, name="bank", tag="stage1", bufs=4)
                for a in range(PASSES):
                    words, scales = operand(a, b, t)
                    nc.tensor.matmul_mx(
                        out=bank[:],
                        lhsT=words,
                        lhsT_scale=scales,
                        rhs=v_w[a][n][:].bitcast(FP8X4),
                        rhs_scale=v_scales[a][:, n * BANK : (n + 1) * BANK],
                        start=(a == 0),
                        stop=(a == PASSES - 1),
                    )
                banks.append(bank)
            return banks

        def w4_operand(a, b, t):
            words = w4_w[b][:, a, :].bitcast(U8)[:, 2 * t * P : 2 * (t + 1) * P]
            return words.bitcast(FP4X4), w4_sc[b][:, a, :].bitcast(U8)[:, t * P : (t + 1) * P]

        def w1_operand(a, b, t):
            words, scales = w1_mx[a, b]
            return words[:, t * P : (t + 1) * P].bitcast(FP8X4), scales[:, t * P : (t + 1) * P]

        h1_planes, h2_planes, c1_planes, c_rows = {}, {}, {}, {}

        def h_tile(b, t):
            if t == 0:
                h1_planes[b] = planes_tile("h1_planes%d" % b, "pos1_planes%d" % b)
                h2_planes[b] = planes_tile("h2_planes%d" % b, "pos2_planes%d" % b)
            banks = stage1(b, t, w4_operand)
            tanh_rows = ring.tile([P, S], F32, name="tanh_rows", tag="rows", bufs=10, align_bytes=64)
            for n, bank in enumerate(banks):
                nc.scalar.activation(
                    tanh_rows[:, n * BANK : (n + 1) * BANK], bank[:], ACT.Tanh, bias=consts[:, b, t : t + 1]
                )
            h_rows = ring.tile([P, S], F32, name="h_rows", bufs=3, align_bytes=64)
            nc.gpsimd.tensor_scalar(
                h_rows[:], tanh_rows[:], consts[:, b, PACK + t : PACK + t + 1], 0.0, ALU.mult, ALU.add
            )
            nc.vector.tensor_copy(h1_planes[b][:, t, :], h_rows[:].indirect(pos1_sb[:]))
            nc.vector.tensor_copy(h2_planes[b][:, t, :], h_rows[:].indirect(pos2_sb[:]))

        def c_tile(b, t):
            banks = stage1(b, t, w1_operand, late=(b == 1 and t >= 2))
            c_rows[b, t] = ring.tile([P, S], F32, name="c_rows", tag="rows", bufs=10, align_bytes=64)
            for n, bank in enumerate(banks):
                nc.scalar.copy(c_rows[b, t][:, n * BANK : (n + 1) * BANK], bank[:])

        def c_gather(b, t, m0=0, m1=NP):
            if b not in c1_planes:
                c1_planes[b] = planes_tile("c1_planes%d" % b, "pos1_planes%d" % b)
            nc.vector.tensor_copy(
                c1_planes[b][:, t, m0:m1], c_rows[b, t][:].indirect(pos1_sb[:, m0 // 16 : m1 // 16])
            )

        def woven(tile, c0=0, c1=BANK):
            return tile[:, PACK * c0 : PACK * c1].rearrange("p (c i t) -> p c t i", i=4, t=PACK)

        def by_fours(planes, c0=0, c1=BANK):
            return planes[:, :, c0:c1].rearrange("p t (c i) -> p c t i", i=4)

        x1_mx, x2_mx, h2_mx, c1_mx = {}, {}, {}, {}

        def x2_operand(b):
            magnitude = load_tile("magnitude", [P, PACK * BANK], F32, 3)
            nc.scalar.activation(woven(magnitude), by_fours(h2_planes[b]), ACT.Abs)
            x2 = rounded_tile("x2_bf%d" % b)
            nc.vector.tensor_tensor(
                x2[:].rearrange("p (m t) -> p m t", t=PACK),
                magnitude[:].rearrange("p (m t) -> p m t", t=PACK),
                consts[:, b, 2 * PACK : 3 * PACK].unsqueeze(1).to_broadcast([P, BANK, PACK]),
                ALU.mult,
            )
            x2_mx[b] = mx_tiles("x2_mx%d" % b)
            quantize(x2_mx[b], x2)

        def plain_operand(name, planes):
            rounded = rounded_tile(name + "_bf")
            nc.scalar.copy(woven(rounded), by_fours(planes))
            mx = mx_tiles(name + "_mx")
            quantize(mx, rounded)
            return mx

        scores = {}

        def stage2(mt, left, right, start, stop):
            nc.tensor.matmul_mx(
                out=scores[mt][:],
                lhsT=left[0][:, mt * P : (mt + 1) * P].bitcast(FP8X4),
                lhsT_scale=left[1][:, mt * P : (mt + 1) * P],
                rhs=right[0][:].bitcast(FP8X4),
                rhs_scale=right[1][:],
                start=start,
                stop=stop,
            )

        def finish(mt):
            squashed = ring.tile([P, NP], F32, name="squashed", bufs=2, align_bytes=64)
            nc.scalar.activation(squashed[:], scores[mt][:], ACT.Tanh)
            result = ring.tile([P, NP], F32, name="result", bufs=2, align_bytes=64)
            nc.vector.tensor_tensor(result[:], squashed[:], review_sb[:, mt, :], ALU.mult)
            nc.sync.dma_start(out[mt * P : (mt + 1) * P, :], result[:])

        first = prepare_w1(0, 0, nc.vector.tensor_copy)
        review_sb = load_tile("review_sb", [P, NP // P, NP], F32, 0)
        nc.sync.dma_start(review_sb[:], review.rearrange("(mt p) j -> p mt j", p=P))
        h_tile(0, 0)
        quantize_w1(0, 0, first)
        h_tile(0, 1)
        quantize_w1(1, 0, prepare_w1(1, 0, nc.scalar.copy))
        h_tile(0, 2)
        h_tile(0, 3)
        quantize_w1(0, 1, prepare_w1(0, 1, nc.scalar.copy))
        h_tile(1, 0)
        quantize_w1(1, 1, prepare_w1(1, 1, nc.scalar.copy))
        h_tile(1, 1)
        x2_operand(0)
        h2_mx[0] = plain_operand("h2_0", h2_planes[0])
        h_tile(1, 2)
        x1_mx[0] = plain_operand("x1_0", h1_planes[0])
        h_tile(1, 3)
        for b in range(GROUPS):
            for t in range(PACK):
                c_tile(b, t)
        for t in range(PACK):
            c_gather(0, t)
        x2_operand(1)
        h2_mx[1] = plain_operand("h2_1", h2_planes[1])
        x1_mx[1] = plain_operand("x1_1", h1_planes[1])
        c1_mx[0] = plain_operand("c1_0", c1_planes[0])
        for mt in range(NP // P):
            scores[mt] = psum.tile([P, NP], F32, name="scores%d" % mt, tag="scores%d" % mt)
        for b in range(GROUPS):
            for mt in range(NP // P):
                stage2(mt, x1_mx[b], x2_mx[b], b == 0, False)
        for mt in range(NP // P):
            stage2(mt, c1_mx[0], h2_mx[0], False, False)
        c1 = rounded_tile("c1_bf1")
        c1_mx[1] = mx_tiles("c1_mx1")
        for m0, m1 in ((0, 256), (256, 384), (384, 512)):
            for t in range(PACK):
                c_gather(1, t, m0, m1)
            nc.vector.tensor_copy(woven(c1, m0, m1), by_fours(c1_planes[1], m0, m1))
            quantize(c1_mx[1], c1, m0, m1)
            for mt in range(m0 // P, m1 // P):
                stage2(mt, c1_mx[1], h2_mx[1], False, True)
                finish(mt)
